import numpy as np
import ml_dtypes


def mxq(x, axis, fmt="e4m3"):
    dtype, down = {"e4m3": (ml_dtypes.float8_e4m3fn, 7), "e5m2": (ml_dtypes.float8_e5m2, 14)}[fmt]
    v = np.moveaxis(np.asarray(x, np.float32).astype(ml_dtypes.bfloat16).astype(np.float64), axis, -1)
    blocks = v.reshape(v.shape[:-1] + (-1, 32))
    amax = np.abs(blocks).max(-1, keepdims=True)
    byte = np.maximum(np.where(amax > 0, np.frexp(amax)[1] - 1 + 127, 0) - down, 1)
    scale = np.exp2(byte - 127.0)
    codes = (blocks / scale).astype(np.float32).astype(dtype).astype(np.float64)
    return np.moveaxis((codes * scale).reshape(v.shape), -1, axis)


WIDE = False


def mx_kscale(k, group=512):
    if not WIDE:
        return np.ones(k)
    levels = np.array([10, -10, 5, -5, 0])
    if group != 512:
        return np.exp2(np.random.permutation(np.resize(levels, k // group))).repeat(group)
    if k % 512:
        return np.exp2(np.random.permutation(np.resize(levels, k // 32))).repeat(32)
    a = np.empty((k // 512, 16))
    for p in range(k // 512):
        a[p, :8] = np.random.permutation(np.resize(levels, 8))
        for g in range(8):
            far = levels[np.abs(levels - a[p, g]) >= 10]
            a[p, g + 8] = far[np.random.randint(len(far))]
    return np.exp2(a.ravel()).repeat(32)


def f64(x):
    return np.asarray(x).astype(np.float64)


G, D, M, O, N = 2, 256, 128, 256, 512


def setup_inputs():
    n = np.random.standard_normal
    s_d = mx_kscale(D, 0)
    s_o = mx_kscale(O, 0)
    return {
        "x": (n((G, D, N)) * s_d[:, None]).astype(np.float32),
        "w1": (n((G, D, M)) / np.sqrt(D) / s_d[:, None]).astype(np.float32),
        "w2": (n((G, D, M)) / np.sqrt(D) / s_d[:, None]).astype(np.float32),
        "tp": (np.random.uniform(0.5, 1.2, (G, M, 1))).astype(np.float32),
        "wo": (n((G, O, M)) / np.sqrt(O) / s_o[:, None]).astype(np.float32),
        "dy": (n((G, O, N)) * s_o[:, None]).astype(np.float32),
        "dx": (n((G, D, N)) * s_d[:, None]).astype(np.float32),
        "og": (np.random.uniform(0.5, 2.0, (G, M, 1))).astype(np.float32),
        "base": (0.3 * n((G, M, N))).astype(np.float32),
    }


def reference(x, w1, w2, tp, wo, dy, dx, og, base):
    w1q = mxq(f64(w1), 1, "e4m3")
    xq = mxq(f64(x), 1, "e4m3")
    z1 = w1q.transpose(0, 2, 1) @ xq
    dxq = mxq(f64(dx), 1, "e4m3")
    tz1 = w1q.transpose(0, 2, 1) @ dxq
    w2q = mxq(f64(w2), 1, "e4m3")
    z2 = w2q.transpose(0, 2, 1) @ xq
    tz2 = w2q.transpose(0, 2, 1) @ dxq
    p1 = np.exp(z1 * f64(tp) - np.max(z1 * f64(tp), axis=-1, keepdims=True))
    zs = np.sum(p1, axis=-1, keepdims=True)
    woq = mxq(f64(wo), 1, "e4m3")
    dyq = mxq(f64(dy), 1, "e4m3")
    c0 = woq.transpose(0, 2, 1) @ dyq
    dzs = np.sum(c0 * 512.0 * z2 * p1 / np.square(zs) * (-1.0), axis=-1, keepdims=True)
    dp1 = c0 * 512.0 * z2 / zs + dzs
    xp1 = tz1 * f64(tp) * p1
    xzs = np.sum(xp1, axis=-1, keepdims=True)
    xdzs = np.sum((tz2 * c0 * 512.0 * p1 + xp1 * c0 * 512.0 * z2 - xzs * zs * 2.0 * c0 * 512.0 * z2 * p1 / np.square(zs)) / np.square(zs) * (-1.0), axis=-1, keepdims=True)
    xdp1 = (tz2 * c0 * 512.0 - xzs * c0 * 512.0 * z2 / zs) / zs + xdzs
    xdz1 = (xdp1 * p1 + xp1 * dp1) * f64(tp)
    y = xdz1 * f64(og) + f64(base)
    return y

@@ -1,0 +1,175 @@
+from contextlib import ExitStack
+
+import concourse.mybir as mybir
+
+G, D, M, N = 2, 256, 128, 512
+FLOPS = 5 * 2 * G * D * M * N
+
+F32 = mybir.dt.float32
+BF16 = mybir.dt.bfloat16
+U32 = mybir.dt.uint32
+U8 = mybir.dt.uint8
+FP8X4 = mybir.dt.float8_e4m3fn_x4
+ALU = mybir.AluOpType
+ACT = mybir.ActivationFunctionType
+
+P = 128
+PACK = 4
+ROWS = D // PACK
+RUN = 4
+X_SPLIT = 320
+DY_SPLIT = 384
+
+
+def tile_rows_hvrowsoft_kernel(tc, x, w1, w2, tp, wo, dy, dx, og, base, out):
+    nc = tc.nc
+    with ExitStack() as ctx:
+        sb = ctx.enter_context(tc.tile_pool(name="sb", bufs=1))
+        psum = ctx.enter_context(tc.psum_pool(name="psum", bufs=1))
+        ctx.enter_context(tc.manual_schedule())
+
+        def operand(name, width):
+            return {
+                "raw": sb.tile([P, PACK, width], F32, name=name + "_raw", align_bytes=64),
+                "packed": sb.tile([P, width, PACK], BF16, name=name + "_packed", align_bytes=64),
+                "codes": sb.tile([P, width], U32, name=name + "_codes", align_bytes=64),
+                "scales": sb.tile([P, width], U8, name=name + "_scales", align_bytes=64),
+            }
+
+        def load(op, src):
+            nc.sync.dma_start(out=op["raw"][:], in_=src.rearrange("g (p j) n -> (g p) j n", j=PACK))
+
+        def pack(copy, op, lo, hi):
+            copy(
+                out=op["packed"][:, lo:hi, :].rearrange("p (c i) j -> p c j i", i=RUN),
+                in_=op["raw"][:, :, lo:hi].rearrange("p j (c i) -> p c j i", i=RUN),
+            )
+
+        def quantize(op):
+            nc.vector.quantize_mx(
+                out=op["codes"][:].bitcast(FP8X4),
+                scales=op["scales"][:],
+                in_=op["packed"][:].rearrange("p n j -> p (n j)"),
+            )
+
+        def product(bank, w, a, g):
+            rows = slice(ROWS * g, ROWS * (g + 1))
+            nc.tensor.matmul_mx(
+                out=bank[:],
+                lhsT=w["codes"][rows, :].bitcast(FP8X4),
+                lhsT_scale=w["scales"][rows, :],
+                rhs=a["codes"][rows, :].bitcast(FP8X4),
+                rhs_scale=a["scales"][rows, :],
+                start=True,
+                stop=True,
+            )
+
+        def wide(name):
+            return [sb.tile([P, N], F32, name="%s%d" % (name, g)) for g in range(G)]
+
+        def banks(name):
+            return [psum.tile([P, N], F32, name="%s%d" % (name, g)) for g in range(G)]
+
+        def stat(name):
+            return sb.tile([P, G], F32, name=name)
+
+        def col(t, g):
+            return t[:, g : g + 1]
+
+        stt = nc.vector.scalar_tensor_tensor
+        xo, dyo, dxo = operand("x", N), operand("dy", N), operand("dx", N)
+        w1o, w2o, woo = operand("w1", M), operand("w2", M), operand("wo", M)
+        base_sb = sb.tile([P, G, N], F32, name="base_sb")
+        rows_in = sb.tile([P, 32], F32, name="rows_in", align_bytes=64)
+        feat = sb.tile([P, 32], F32, name="feat", align_bytes=64)
+        z1, c0, z2, tz2 = banks("z1"), banks("c0"), banks("z2"), banks("tz2")
+        tz1 = z1
+        neg_score, p, q, a, e1, b, pt, e2, zb, xs, y = [
+            wide(name) for name in ("neg_score", "p", "q", "a", "e1", "b", "pt", "e2", "zb", "xs", "y")
+        ]
+        neg_tp, gain, neg_max, zs, rz, gq, sum_a, mean_a, mean_t, sum_b, sum_e2, cc = [
+            stat(name)
+            for name in ("neg_tp", "gain", "neg_max", "zs", "rz", "gq", "sum_a", "mean_a", "mean_t", "sum_b", "sum_e2", "cc")
+        ]
+        warm = sb.tile([P, 1], F32, name="warm")
+
+        zero = sb.tile([P, 1], F32, name="zero")
+        nc.vector.memset(rows_in[:], 0.0)
+        nc.vector.memset(zero[:], 0.0)
+        load(xo, x)
+        nc.sync.dma_start(out=rows_in[0:P:16, :], in_=tp.rearrange("g (q c) o -> q g (c o)", c=32))
+        nc.sync.dma_start(out=rows_in[1:P:16, :], in_=og.rearrange("g (q c) o -> q g (c o)", c=32))
+        load(w1o, w1)
+        load(woo, wo)
+        load(dyo, dy)
+        load(w2o, w2)
+        load(dxo, dx)
+        nc.sync.dma_start(out=base_sb[:], in_=base.rearrange("g m n -> m g n"))
+        nc.scalar.activation(out=warm[:], in_=zero[:], func=ACT.Exp)
+
+        pack(nc.vector.tensor_copy, xo, 0, X_SPLIT)
+        pack(nc.scalar.copy, xo, X_SPLIT, N)
+        pack(nc.scalar.copy, w1o, 0, M)
+        pack(nc.scalar.copy, woo, 0, M)
+        nc.vector.transpose(out=feat[:], in_=rows_in[:])
+        quantize(xo)
+        quantize(w1o)
+        quantize(woo)
+        tp_sb = feat[:, 0:32:16]
+        og_sb = feat[:, 1:32:16]
+        nc.vector.tensor_scalar(out=neg_tp[:], in0=tp_sb, scalar1=-1.0, scalar2=None, op0=ALU.mult)
+        stt(out=gain[:], in0=tp_sb, scalar=float(N), in1=og_sb, op0=ALU.mult, op1=ALU.mult)
+
+        for g in range(G):
+            product(z1[g], w1o, xo, g)
+        for g in range(G):
+            nc.vector.tensor_scalar(
+                out=neg_score[g][:], in0=z1[g][:], scalar1=col(neg_tp, g), scalar2=None,
+                op0=ALU.mult, op1=ALU.min, accum_out=col(neg_max, g),
+            )
+            nc.scalar.activation(
+                out=p[g][:], in_=neg_score[g][:], func=ACT.Exp, scale=-1.0, bias=col(neg_max, g), accum_out=col(zs, g)
+            )
+
+        pack(nc.vector.tensor_copy, dyo, 0, DY_SPLIT)
+        pack(nc.scalar.copy, dyo, DY_SPLIT, N)
+        pack(nc.scalar.copy, w2o, 0, M)
+        nc.vector.reciprocal(out=rz[:], in_=zs[:])
+        quantize(dyo)
+        nc.vector.tensor_tensor(out=gq[:], in0=gain[:], in1=rz[:], op=ALU.mult)
+        quantize(w2o)
+        for g in range(G):
+            product(c0[g], woo, dyo, g)
+        for g in range(G):
+            product(z2[g], w2o, xo, g)
+        pack(nc.scalar.copy, dxo, 0, N)
+
+        for g in range(G):
+            stt(out=q[g][:], in0=c0[g][:], scalar=col(gq, g), in1=p[g][:], op0=ALU.mult, op1=ALU.mult)
+        for g in range(G):
+            stt(out=a[g][:], in0=z2[g][:], scalar=feat[:, 16 * g : 16 * g + 1], in1=q[g][:], op0=ALU.mult, op1=ALU.mult,
+                accum_out=col(sum_a, g))
+        quantize(dxo)
+        nc.vector.tensor_tensor(out=mean_a[:], in0=sum_a[:], in1=rz[:], op=ALU.mult)
+        for g in range(G):
+            product(tz2[g], w2o, dxo, g)
+        for g in range(G):
+            product(tz1[g], w1o, dxo, g)
+        for g in range(G):
+            stt(out=e1[g][:], in0=p[g][:], scalar=col(mean_a, g), in1=a[g][:], op0=ALU.mult, op1=ALU.subtract)
+        for g in range(G):
+            stt(out=b[g][:], in0=tz2[g][:], scalar=1.0, in1=q[g][:], op0=ALU.mult, op1=ALU.mult, accum_out=col(sum_b, g))
+        for g in range(G):
+            stt(out=pt[g][:], in0=tz1[g][:], scalar=col(rz, g), in1=p[g][:], op0=ALU.mult, op1=ALU.mult,
+                accum_out=col(mean_t, g))
+        for g in range(G):
+            stt(out=e2[g][:], in0=tz1[g][:], scalar=col(mean_t, g), in1=e1[g][:], op0=ALU.subtract, op1=ALU.mult,
+                accum_out=col(sum_e2, g))
+        for g in range(G):
+            nc.vector.tensor_tensor(out=zb[g][:], in0=b[g][:], in1=base_sb[:, g, :], op=ALU.add)
+            stt(out=col(cc, g), in0=col(sum_b, g), scalar=col(sum_e2, g), in1=col(rz, g), op0=ALU.subtract, op1=ALU.mult)
+        for g in range(G):
+            stt(out=xs[g][:], in0=p[g][:], scalar=col(cc, g), in1=e2[g][:], op0=ALU.mult, op1=ALU.add)
+        for g in range(G):
+            nc.vector.tensor_tensor(out=y[g][:], in0=zb[g][:], in1=xs[g][:], op=ALU.subtract)
+            nc.sync.dma_start(out=out[g], in_=y[g][:])

@@ -17,8 +17,8 @@ P = 128
 PACK = 4
 ROWS = D // PACK
 RUN = 4
-X_SPLIT = 320
-DY_SPLIT = 384
+X_SPLIT = 368
+DY_SPLIT = 304
 
 
 def tile_rows_hvrowsoft_kernel(tc, x, w1, w2, tp, wo, dy, dx, og, base, out):
@@ -87,25 +87,21 @@ def tile_rows_hvrowsoft_kernel(tc, x, w1, w2, tp, wo, dy, dx, og, base, out):
         neg_score, p, q, a, e1, b, pt, e2, zb, xs, y = [
             wide(name) for name in ("neg_score", "p", "q", "a", "e1", "b", "pt", "e2", "zb", "xs", "y")
         ]
-        neg_tp, gain, neg_max, zs, rz, gq, sum_a, mean_a, mean_t, sum_b, sum_e2, cc = [
+        neg_tp, gain, neg_max, zs, rz, tprz, sum_a, mean_a, mean_t, sum_b, sum_e2, cc, mean_b = [
             stat(name)
-            for name in ("neg_tp", "gain", "neg_max", "zs", "rz", "gq", "sum_a", "mean_a", "mean_t", "sum_b", "sum_e2", "cc")
+            for name in ("neg_tp", "gain", "neg_max", "zs", "rz", "tprz", "sum_a", "mean_a", "mean_t", "sum_b", "sum_e2", "cc", "mean_b")
         ]
-        warm = sb.tile([P, 1], F32, name="warm")
 
-        zero = sb.tile([P, 1], F32, name="zero")
         nc.vector.memset(rows_in[:], 0.0)
-        nc.vector.memset(zero[:], 0.0)
         load(xo, x)
+        load(w1o, w1)
         nc.sync.dma_start(out=rows_in[0:P:16, :], in_=tp.rearrange("g (q c) o -> q g (c o)", c=32))
         nc.sync.dma_start(out=rows_in[1:P:16, :], in_=og.rearrange("g (q c) o -> q g (c o)", c=32))
-        load(w1o, w1)
         load(woo, wo)
         load(dyo, dy)
         load(w2o, w2)
         load(dxo, dx)
         nc.sync.dma_start(out=base_sb[:], in_=base.rearrange("g m n -> m g n"))
-        nc.scalar.activation(out=warm[:], in_=zero[:], func=ACT.Exp)
 
         pack(nc.vector.tensor_copy, xo, 0, X_SPLIT)
         pack(nc.scalar.copy, xo, X_SPLIT, N)
@@ -118,58 +114,85 @@ def tile_rows_hvrowsoft_kernel(tc, x, w1, w2, tp, wo, dy, dx, og, base, out):
         tp_sb = feat[:, 0:32:16]
         og_sb = feat[:, 1:32:16]
         nc.vector.tensor_scalar(out=neg_tp[:], in0=tp_sb, scalar1=-1.0, scalar2=None, op0=ALU.mult)
-        stt(out=gain[:], in0=tp_sb, scalar=float(N), in1=og_sb, op0=ALU.mult, op1=ALU.mult)
+        stt(out=gain[:], in0=tp_sb, scalar=-float(N), in1=og_sb, op0=ALU.mult, op1=ALU.mult)
 
         for g in range(G):
             product(z1[g], w1o, xo, g)
-        for g in range(G):
+
+        def row_max(g):
             nc.vector.tensor_scalar(
                 out=neg_score[g][:], in0=z1[g][:], scalar1=col(neg_tp, g), scalar2=None,
                 op0=ALU.mult, op1=ALU.min, accum_out=col(neg_max, g),
             )
+
+        def exp(g):
             nc.scalar.activation(
                 out=p[g][:], in_=neg_score[g][:], func=ACT.Exp, scale=-1.0, bias=col(neg_max, g), accum_out=col(zs, g)
             )
 
+        def scaled(dst, src, scale):
+            nc.scalar.activation(out=dst, in_=src, func=ACT.Copy, scale=scale)
+
+        def make_q(g):
+            stt(out=q[g][:], in0=c0[g][:], scalar=col(gain, g), in1=p[g][:], op0=ALU.mult, op1=ALU.mult)
+
+        def make_a(g):
+            stt(out=a[g][:], in0=z2[g][:], scalar=col(rz, g), in1=q[g][:], op0=ALU.mult, op1=ALU.mult,
+                accum_out=col(sum_a, g))
+
+        row_max(0)
         pack(nc.vector.tensor_copy, dyo, 0, DY_SPLIT)
         pack(nc.scalar.copy, dyo, DY_SPLIT, N)
-        pack(nc.scalar.copy, w2o, 0, M)
-        nc.vector.reciprocal(out=rz[:], in_=zs[:])
+        exp(0)
+        row_max(1)
+        exp(1)
         quantize(dyo)
-        nc.vector.tensor_tensor(out=gq[:], in0=gain[:], in1=rz[:], op=ALU.mult)
-        quantize(w2o)
         for g in range(G):
             product(c0[g], woo, dyo, g)
+        pack(nc.vector.tensor_copy, w2o, 0, M)
+        nc.vector.reciprocal(out=col(rz, 0), in_=col(zs, 0))
+        quantize(w2o)
         for g in range(G):
             product(z2[g], w2o, xo, g)
         pack(nc.scalar.copy, dxo, 0, N)
-
-        for g in range(G):
-            stt(out=q[g][:], in0=c0[g][:], scalar=col(gq, g), in1=p[g][:], op0=ALU.mult, op1=ALU.mult)
-        for g in range(G):
-            stt(out=a[g][:], in0=z2[g][:], scalar=feat[:, 16 * g : 16 * g + 1], in1=q[g][:], op0=ALU.mult, op1=ALU.mult,
-                accum_out=col(sum_a, g))
+        make_q(0)
+        make_q(1)
+        nc.vector.reciprocal(out=col(rz, 1), in_=col(zs, 1))
+        make_a(0)
+        make_a(1)
         quantize(dxo)
-        nc.vector.tensor_tensor(out=mean_a[:], in0=sum_a[:], in1=rz[:], op=ALU.mult)
         for g in range(G):
             product(tz2[g], w2o, dxo, g)
         for g in range(G):
             product(tz1[g], w1o, dxo, g)
         for g in range(G):
+            scaled(col(tprz, g), col(neg_tp, g), col(rz, g))
+            scaled(col(mean_a, g), col(sum_a, g), col(rz, g))
+        for g in range(G):
             stt(out=e1[g][:], in0=p[g][:], scalar=col(mean_a, g), in1=a[g][:], op0=ALU.mult, op1=ALU.subtract)
         for g in range(G):
-            stt(out=b[g][:], in0=tz2[g][:], scalar=1.0, in1=q[g][:], op0=ALU.mult, op1=ALU.mult, accum_out=col(sum_b, g))
+            stt(out=b[g][:], in0=tz2[g][:], scalar=col(rz, g), in1=q[g][:], op0=ALU.mult, op1=ALU.mult,
+                accum_out=col(sum_b, g))
+            nc.gpsimd.tensor_tensor(out=zb[g][:], in0=base_sb[:, g, :], in1=b[g][:], op=ALU.subtract)
+            scaled(col(mean_b, g), col(sum_b, g), col(rz, g))
         for g in range(G):
             stt(out=pt[g][:], in0=tz1[g][:], scalar=col(rz, g), in1=p[g][:], op0=ALU.mult, op1=ALU.mult,
                 accum_out=col(mean_t, g))
         for g in range(G):
             stt(out=e2[g][:], in0=tz1[g][:], scalar=col(mean_t, g), in1=e1[g][:], op0=ALU.subtract, op1=ALU.mult,
                 accum_out=col(sum_e2, g))
-        for g in range(G):
-            nc.vector.tensor_tensor(out=zb[g][:], in0=b[g][:], in1=base_sb[:, g, :], op=ALU.add)
-            stt(out=col(cc, g), in0=col(sum_b, g), scalar=col(sum_e2, g), in1=col(rz, g), op0=ALU.subtract, op1=ALU.mult)
-        for g in range(G):
-            stt(out=xs[g][:], in0=p[g][:], scalar=col(cc, g), in1=e2[g][:], op0=ALU.mult, op1=ALU.add)
-        for g in range(G):
-            nc.vector.tensor_tensor(out=y[g][:], in0=zb[g][:], in1=xs[g][:], op=ALU.subtract)
-            nc.sync.dma_start(out=out[g], in_=y[g][:])
+            nc.scalar.activation(out=col(cc, g), in_=col(sum_e2, g), func=ACT.Identity, scale=col(tprz, g), bias=col(mean_b, g))
+
+        def gather_terms(g, lo, hi):
+            stt(out=xs[g][:, lo:hi], in0=e2[g][:, lo:hi], scalar=col(tp_sb, g), in1=zb[g][:, lo:hi], op0=ALU.mult, op1=ALU.add)
+
+        def finish(g, lo, hi):
+            stt(out=y[g][:, lo:hi], in0=p[g][:, lo:hi], scalar=col(cc, g), in1=xs[g][:, lo:hi], op0=ALU.mult, op1=ALU.add)
+            nc.sync.dma_start(out=out[g, :, lo:hi], in_=y[g][:, lo:hi])
+
+        gather_terms(0, 0, N)
+        gather_terms(1, 0, N // 2)
+        finish(0, 0, N)
+        gather_terms(1, N // 2, N)
+        finish(1, 0, N // 2)
+        finish(1, N // 2, N)

from contextlib import ExitStack

import concourse.mybir as mybir

G, D, M, N = 2, 256, 128, 512
FLOPS = 5 * 2 * G * D * M * N

F32 = mybir.dt.float32
BF16 = mybir.dt.bfloat16
U32 = mybir.dt.uint32
U8 = mybir.dt.uint8
FP8X4 = mybir.dt.float8_e4m3fn_x4
ALU = mybir.AluOpType
ACT = mybir.ActivationFunctionType

P = 128
PACK = 4
ROWS = D // PACK
RUN = 4
X_SPLIT = 368
DY_SPLIT = 304


def tile_rows_hvrowsoft_kernel(tc, x, w1, w2, tp, wo, dy, dx, og, base, out):
    nc = tc.nc
    with ExitStack() as ctx:
        sb = ctx.enter_context(tc.tile_pool(name="sb", bufs=1))
        psum = ctx.enter_context(tc.psum_pool(name="psum", bufs=1))
        ctx.enter_context(tc.manual_schedule())

        def operand(name, width):
            return {
                "raw": sb.tile([P, PACK, width], F32, name=name + "_raw", align_bytes=64),
                "packed": sb.tile([P, width, PACK], BF16, name=name + "_packed", align_bytes=64),
                "codes": sb.tile([P, width], U32, name=name + "_codes", align_bytes=64),
                "scales": sb.tile([P, width], U8, name=name + "_scales", align_bytes=64),
            }

        def load(op, src):
            nc.sync.dma_start(out=op["raw"][:], in_=src.rearrange("g (p j) n -> (g p) j n", j=PACK))

        def pack(copy, op, lo, hi):
            copy(
                out=op["packed"][:, lo:hi, :].rearrange("p (c i) j -> p c j i", i=RUN),
                in_=op["raw"][:, :, lo:hi].rearrange("p j (c i) -> p c j i", i=RUN),
            )

        def quantize(op):
            nc.vector.quantize_mx(
                out=op["codes"][:].bitcast(FP8X4),
                scales=op["scales"][:],
                in_=op["packed"][:].rearrange("p n j -> p (n j)"),
            )

        def product(bank, w, a, g):
            rows = slice(ROWS * g, ROWS * (g + 1))
            nc.tensor.matmul_mx(
                out=bank[:],
                lhsT=w["codes"][rows, :].bitcast(FP8X4),
                lhsT_scale=w["scales"][rows, :],
                rhs=a["codes"][rows, :].bitcast(FP8X4),
                rhs_scale=a["scales"][rows, :],
                start=True,
                stop=True,
            )

        def wide(name):
            return [sb.tile([P, N], F32, name="%s%d" % (name, g)) for g in range(G)]

        def banks(name):
            return [psum.tile([P, N], F32, name="%s%d" % (name, g)) for g in range(G)]

        def stat(name):
            return sb.tile([P, G], F32, name=name)

        def col(t, g):
            return t[:, g : g + 1]

        stt = nc.vector.scalar_tensor_tensor
        xo, dyo, dxo = operand("x", N), operand("dy", N), operand("dx", N)
        w1o, w2o, woo = operand("w1", M), operand("w2", M), operand("wo", M)
        base_sb = sb.tile([P, G, N], F32, name="base_sb")
        rows_in = sb.tile([P, 32], F32, name="rows_in", align_bytes=64)
        feat = sb.tile([P, 32], F32, name="feat", align_bytes=64)
        z1, c0, z2, tz2 = banks("z1"), banks("c0"), banks("z2"), banks("tz2")
        tz1 = z1
        neg_score, p, q, a, e1, b, pt, e2, zb, xs, y = [
            wide(name) for name in ("neg_score", "p", "q", "a", "e1", "b", "pt", "e2", "zb", "xs", "y")
        ]
        neg_tp, gain, neg_max, zs, rz, tprz, sum_a, mean_a, mean_t, sum_b, sum_e2, cc, mean_b = [
            stat(name)
            for name in ("neg_tp", "gain", "neg_max", "zs", "rz", "tprz", "sum_a", "mean_a", "mean_t", "sum_b", "sum_e2", "cc", "mean_b")
        ]

        nc.vector.memset(rows_in[:], 0.0)
        load(xo, x)
        load(w1o, w1)
        nc.sync.dma_start(out=rows_in[0:P:16, :], in_=tp.rearrange("g (q c) o -> q g (c o)", c=32))
        nc.sync.dma_start(out=rows_in[1:P:16, :], in_=og.rearrange("g (q c) o -> q g (c o)", c=32))
        load(woo, wo)
        load(dyo, dy)
        load(w2o, w2)
        load(dxo, dx)
        nc.sync.dma_start(out=base_sb[:], in_=base.rearrange("g m n -> m g n"))

        pack(nc.vector.tensor_copy, xo, 0, X_SPLIT)
        pack(nc.scalar.copy, xo, X_SPLIT, N)
        pack(nc.scalar.copy, w1o, 0, M)
        pack(nc.scalar.copy, woo, 0, M)
        nc.vector.transpose(out=feat[:], in_=rows_in[:])
        quantize(xo)
        quantize(w1o)
        quantize(woo)
        tp_sb = feat[:, 0:32:16]
        og_sb = feat[:, 1:32:16]
        nc.vector.tensor_scalar(out=neg_tp[:], in0=tp_sb, scalar1=-1.0, scalar2=None, op0=ALU.mult)
        stt(out=gain[:], in0=tp_sb, scalar=-float(N), in1=og_sb, op0=ALU.mult, op1=ALU.mult)

        for g in range(G):
            product(z1[g], w1o, xo, g)

        def row_max(g):
            nc.vector.tensor_scalar(
                out=neg_score[g][:], in0=z1[g][:], scalar1=col(neg_tp, g), scalar2=None,
                op0=ALU.mult, op1=ALU.min, accum_out=col(neg_max, g),
            )

        def exp(g):
            nc.scalar.activation(
                out=p[g][:], in_=neg_score[g][:], func=ACT.Exp, scale=-1.0, bias=col(neg_max, g), accum_out=col(zs, g)
            )

        def scaled(dst, src, scale):
            nc.scalar.activation(out=dst, in_=src, func=ACT.Copy, scale=scale)

        def make_q(g):
            stt(out=q[g][:], in0=c0[g][:], scalar=col(gain, g), in1=p[g][:], op0=ALU.mult, op1=ALU.mult)

        def make_a(g):
            stt(out=a[g][:], in0=z2[g][:], scalar=col(rz, g), in1=q[g][:], op0=ALU.mult, op1=ALU.mult,
                accum_out=col(sum_a, g))

        row_max(0)
        pack(nc.vector.tensor_copy, dyo, 0, DY_SPLIT)
        pack(nc.scalar.copy, dyo, DY_SPLIT, N)
        exp(0)
        row_max(1)
        exp(1)
        quantize(dyo)
        for g in range(G):
            product(c0[g], woo, dyo, g)
        pack(nc.vector.tensor_copy, w2o, 0, M)
        nc.vector.reciprocal(out=col(rz, 0), in_=col(zs, 0))
        quantize(w2o)
        for g in range(G):
            product(z2[g], w2o, xo, g)
        pack(nc.scalar.copy, dxo, 0, N)
        make_q(0)
        make_q(1)
        nc.vector.reciprocal(out=col(rz, 1), in_=col(zs, 1))
        make_a(0)
        make_a(1)
        quantize(dxo)
        for g in range(G):
            product(tz2[g], w2o, dxo, g)
        for g in range(G):
            product(tz1[g], w1o, dxo, g)
        for g in range(G):
            scaled(col(tprz, g), col(neg_tp, g), col(rz, g))
            scaled(col(mean_a, g), col(sum_a, g), col(rz, g))
        for g in range(G):
            stt(out=e1[g][:], in0=p[g][:], scalar=col(mean_a, g), in1=a[g][:], op0=ALU.mult, op1=ALU.subtract)
        for g in range(G):
            stt(out=b[g][:], in0=tz2[g][:], scalar=col(rz, g), in1=q[g][:], op0=ALU.mult, op1=ALU.mult,
                accum_out=col(sum_b, g))
            nc.gpsimd.tensor_tensor(out=zb[g][:], in0=base_sb[:, g, :], in1=b[g][:], op=ALU.subtract)
            scaled(col(mean_b, g), col(sum_b, g), col(rz, g))
        for g in range(G):
            stt(out=pt[g][:], in0=tz1[g][:], scalar=col(rz, g), in1=p[g][:], op0=ALU.mult, op1=ALU.mult,
                accum_out=col(mean_t, g))
        for g in range(G):
            stt(out=e2[g][:], in0=tz1[g][:], scalar=col(mean_t, g), in1=e1[g][:], op0=ALU.subtract, op1=ALU.mult,
                accum_out=col(sum_e2, g))
            nc.scalar.activation(out=col(cc, g), in_=col(sum_e2, g), func=ACT.Identity, scale=col(tprz, g), bias=col(mean_b, g))

        def gather_terms(g, lo, hi):
            stt(out=xs[g][:, lo:hi], in0=e2[g][:, lo:hi], scalar=col(tp_sb, g), in1=zb[g][:, lo:hi], op0=ALU.mult, op1=ALU.add)

        def finish(g, lo, hi):
            stt(out=y[g][:, lo:hi], in0=p[g][:, lo:hi], scalar=col(cc, g), in1=xs[g][:, lo:hi], op0=ALU.mult, op1=ALU.add)
            nc.sync.dma_start(out=out[g, :, lo:hi], in_=y[g][:, lo:hi])

        gather_terms(0, 0, N)
        gather_terms(1, 0, N // 2)
        finish(0, 0, N)
        gather_terms(1, N // 2, N)
        finish(1, 0, N // 2)
        finish(1, N // 2, N)
